import numpy as np
import ml_dtypes


def mxq(x, axis, fmt="e4m3"):
    dtype, down = {"e4m3": (ml_dtypes.float8_e4m3fn, 7), "e5m2": (ml_dtypes.float8_e5m2, 14)}[fmt]
    v = np.moveaxis(np.asarray(x, np.float32).astype(ml_dtypes.bfloat16).astype(np.float64), axis, -1)
    blocks = v.reshape(v.shape[:-1] + (-1, 32))
    amax = np.abs(blocks).max(-1, keepdims=True)
    byte = np.maximum(np.where(amax > 0, np.frexp(amax)[1] - 1 + 127, 0) - down, 1)
    scale = np.exp2(byte - 127.0)
    codes = (blocks / scale).astype(np.float32).astype(dtype).astype(np.float64)
    return np.moveaxis((codes * scale).reshape(v.shape), -1, axis)


WIDE = False


def mx_kscale(k):
    if not WIDE:
        return np.ones(k)
    levels = np.array([24, -24, 12, -12, 0])
    if k % 512:
        return np.exp2(np.random.permutation(np.resize(levels, k // 32))).repeat(32)
    a = np.empty((k // 512, 16))
    for p in range(k // 512):
        a[p, :8] = np.random.permutation(np.resize(levels, 8))
        for g in range(8):
            far = levels[np.abs(levels - a[p, g]) >= 10]
            a[p, g + 8] = far[np.random.randint(len(far))]
    return np.exp2(a.ravel()).repeat(32)


def f64(x):
    return np.asarray(x).astype(np.float64)


def striped(idx):
    return np.tile(idx.reshape(-1, 16).T, (8, 1)).astype(np.uint16)


def unstriped(offs):
    return offs[:16].T.reshape(-1).astype(np.int64)


E2M1 = np.array([0.0, 0.5, 1.0, 1.5, 2.0, 3.0, 4.0, 6.0, -0.0, -0.5, -1.0, -1.5, -2.0, -3.0, -4.0, -6.0])


def pack_weight(w, fmt):
    k, n = w.shape
    w = f64(np.asarray(w, np.float32).astype(ml_dtypes.bfloat16)).reshape(k // 32, 32, n)
    amax = np.abs(w).max(1)
    if fmt == "e4m3":
        byte = np.frexp(amax)[1] - 1 + 127 - 7
    else:
        mant, ex = np.frexp(amax / 6.0)
        byte = np.where(mant > 0.5, ex, ex - 1) + 127
    byte = np.clip(np.where(amax > 0, byte, 1), 1, 254)
    scaled = (w * np.exp2(127.0 - byte)[:, None, :]).reshape(k, n).astype(np.float32)
    by_word = np.ascontiguousarray(scaled.reshape(k // 512, 128, 4, n).transpose(0, 1, 3, 2))
    if fmt == "e4m3":
        words = by_word.astype(ml_dtypes.float8_e4m3fn).view(np.uint8)
    else:
        c = by_word.astype(ml_dtypes.float4_e2m1fn).view(np.uint8) & 0xF
        words = (c[..., 0::2] | (c[..., 1::2] << 4)).reshape(k // 512, 128, 2 * n)
    return np.ascontiguousarray(words), np.ascontiguousarray(byte.astype(np.uint8).reshape(k // 512, 16, n))


def unpack_weight(words, scales, fmt):
    g, _, n = scales.shape
    words = np.ascontiguousarray(words).reshape(g, 128, n, -1)
    if fmt == "e4m3":
        vals = words.view(ml_dtypes.float8_e4m3fn).astype(np.float64)
    else:
        nib = np.empty((g, 128, n, 4), np.uint8)
        nib[..., 0::2] = words & 0xF
        nib[..., 1::2] = words >> 4
        vals = E2M1[nib]
    vals = vals * np.repeat(np.exp2(scales.astype(np.float64) - 127.0), 8, axis=1)[..., None]
    return vals.transpose(0, 1, 3, 2).reshape(g * 512, n)


def pack_table4(v):
    words, scales = pack_weight(v, "e2m1")
    g, t = words.shape[0] // 2, v.shape[1]
    return np.ascontiguousarray(words.reshape(g, 2, 128, t, 2).transpose(0, 2, 3, 1, 4).reshape(g, 128, t, 4)), scales


def unpack_table4(words, scales):
    g, _, t, _ = words.shape
    return unpack_weight(words.reshape(g, 128, t, 2, 2).transpose(0, 3, 1, 2, 4).reshape(2 * g, 128, 2 * t), scales, "e2m1")


def sigm(f):
    return 1.0 / (1.0 + np.exp(-np.maximum(f, -700.0)))


K, M, N, T, J = 512, 1024, 1024, 2048, 1024


def setup_inputs():
    n = np.random.standard_normal
    s = mx_kscale(K)[:, None]
    s2 = mx_kscale(M)[:, None]
    h = np.tanh(n((N, T)))
    p_tab = pack_table4(h * s2)
    p_uz = pack_weight(n((M, N)) / np.sqrt(M) / s2, "e2m1")
    p_un = pack_weight(n((M, N)) / np.sqrt(M) / s2, "e2m1")
    return {
        "x": (n((K, J)) * s).astype(np.float32),
        "tab_words": p_tab[0],
        "tab_scales": p_tab[1],
        "wz": (n((K, N)) / np.sqrt(K) / s).astype(np.float32),
        "uz_words": p_uz[0],
        "uz_scales": p_uz[1],
        "wn": (n((K, N)) / np.sqrt(K) / s).astype(np.float32),
        "un_words": p_un[0],
        "un_scales": p_un[1],
        "bz": (0.3 * n(N)).astype(np.float32),
        "bn": (0.3 * n(N)).astype(np.float32),
        "hT": (h).astype(np.float32),
        "wgo": np.tile(np.random.uniform(0.5, 2.0, J), (128, 1)).astype(np.float32),
        "offs": striped(np.random.permutation(T)[:J]),
    }


def reference(x, tab_words, tab_scales, wz, uz_words, uz_scales, wn, un_words, un_scales, bz, bn, hT, wgo, offs):
    idx = unstriped(offs)
    x_ = mxq(f64(x), 0, "e4m3")
    tab_ = unpack_table4(tab_words, tab_scales)[:, idx]
    wz_ = mxq(f64(wz), 0, "e4m3")
    uz_ = unpack_weight(uz_words, uz_scales, "e2m1")
    wn_ = mxq(f64(wn), 0, "e4m3")
    un_ = unpack_weight(un_words, un_scales, "e2m1")
    sz = wz_.T @ x_ + uz_.T @ tab_
    z = sigm(sz + f64(bz)[:, None])
    xn = wn_.T @ x_
    hn = un_.T @ tab_
    cd = np.tanh(xn + f64(bn)[:, None] + z * hn)
    out = np.zeros((N, T))
    out[:, idx] = f64(wgo)[0] * (f64(hT)[:, idx] + z * (cd - f64(hT)[:, idx]))
    return out

@@ -1,0 +1,208 @@
+from contextlib import ExitStack
+
+import concourse.mybir as mybir
+
+K, M, N, T, J = 512, 1024, 1024, 2048, 1024
+FLOPS = 2 * 2 * (K + M) * N * J
+
+F32 = mybir.dt.float32
+BF16 = mybir.dt.bfloat16
+I32 = mybir.dt.int32
+U32 = mybir.dt.uint32
+U16 = mybir.dt.uint16
+U8 = mybir.dt.uint8
+FP8X4 = mybir.dt.float8_e4m3fn_x4
+FP4X4 = mybir.dt.float4_e2m1fn_x4
+ALU = mybir.AluOpType
+ACT = mybir.ActivationFunctionType
+
+P = 128
+PACK = 4
+HALF = 512
+W_PIECE = 256
+CHUNKS = N // P
+AHEAD = 2
+
+
+def tile_list_tgn_mgu_kernel(
+    tc, x, tab_words, tab_scales, wz, uz_words, uz_scales, wn, un_words, un_scales, bz, bn, hT, wgo, offs, out
+):
+    nc = tc.nc
+    with ExitStack() as ctx:
+        keep = ctx.enter_context(tc.tile_pool(name="keep", bufs=1))
+        ring = ctx.enter_context(tc.tile_pool(name="ring", bufs=3))
+        psum = ctx.enter_context(tc.psum_pool(name="psum", bufs=1))
+
+        offsets = keep.tile([P, J // 16], U16, name="offsets")
+        nc.sync.dma_start(offsets[:], offs)
+        table_words = keep.tile([P, T], U32, name="table_words")
+        nc.sync.dma_start(table_words[:].bitcast(I32), tab_words[0].rearrange("p t b -> p (t b)").bitcast(I32))
+
+        def cleared_planes(name, width):
+            planes = keep.tile([P, 2, width], U8, name=name, align_bytes=64)
+            nc.vector.memset(planes[:].bitcast(I32), 0)
+            return planes
+
+        def load_scale_rows(planes, scales):
+            for q in range(4):
+                nc.sync.dma_start(
+                    planes[32 * q : 32 * q + 4].bitcast(I32),
+                    scales[:, 4 * q : 4 * q + 4, :].bitcast(I32).rearrange("a r n -> r a n"),
+                )
+
+        table_planes = cleared_planes("table_planes", T)
+        uz_planes = cleared_planes("uz_planes", N)
+        un_planes = cleared_planes("un_planes", N)
+        load_scale_rows(table_planes, tab_scales)
+
+        pages = []
+        for b in range(2):
+            page = keep.tile([P, T], F32, name="page%d" % b)
+            nc.gpsimd.memset(page[:], 0.0)
+            pages.append(page)
+
+        def load_rows(name, src, cols):
+            raw = keep.tile([P, PACK, cols.stop - cols.start], F32, name=name)
+            nc.sync.dma_start(raw[:], src[:, cols].rearrange("(p i) c -> p i c", i=PACK))
+            return raw
+
+        def load_words(name, words):
+            tile = keep.tile([P, 2, 2 * N], U8, name=name, align_bytes=64)
+            nc.sync.dma_start(tile[:].bitcast(I32), words.bitcast(I32).rearrange("a p n -> p a n"))
+            return tile
+
+        def load_state(c):
+            rows = keep.tile([P, T], F32, name="state%d" % c)
+            nc.sync.dma_start(rows[:], hT[c * P : (c + 1) * P, :])
+            return rows
+
+        def piece(i):
+            return slice(i * W_PIECE, (i + 1) * W_PIECE)
+
+        x_raw = [load_rows("x_raw0", x, slice(0, HALF))]
+        wz_raw = [load_rows("wz_raw0", wz, piece(0))]
+        load_scale_rows(uz_planes, uz_scales)
+        uz_codes = load_words("uz_codes", uz_words)
+        wn_raw = [load_rows("wn_raw0", wn, piece(0))]
+        un_codes = load_words("un_codes", un_words)
+        x_raw.append(load_rows("x_raw1", x, slice(HALF, J)))
+        load_scale_rows(un_planes, un_scales)
+        bz_cols = keep.tile([P, CHUNKS], F32, name="bz_cols")
+        bn_cols = keep.tile([P, CHUNKS], F32, name="bn_cols")
+        with nc.allow_non_contiguous_dma(reason="one bias value a partition"):
+            nc.sync.dma_start(bz_cols[:], bz.rearrange("(c p) -> p c", p=P))
+            nc.sync.dma_start(bn_cols[:], bn.rearrange("(c p) -> p c", p=P))
+        bz_negated = keep.tile([P, CHUNKS], F32, name="bz_negated")
+        nc.scalar.activation(bz_negated[:], bz_cols[:], ACT.Copy, scale=-1.0)
+        states = [load_state(0)]
+        weight = keep.tile([P, J], F32, name="weight")
+        nc.sync.dma_start(weight[:], wgo)
+        states.append(load_state(1))
+        for i in range(1, N // W_PIECE):
+            wz_raw.append(load_rows("wz_raw%d" % i, wz, piece(i)))
+            wn_raw.append(load_rows("wn_raw%d" % i, wn, piece(i)))
+            states.append(load_state(2 * i))
+            states.append(load_state(2 * i + 1))
+
+        picked_words = keep.tile([P, J], U32, name="picked_words")
+        nc.vector.tensor_copy(picked_words[:], table_words[:].indirect(offsets[:]))
+        v_codes = keep.tile([P, 2, 2 * J], U8, name="v_codes", align_bytes=64)
+        nc.vector.tensor_copy(
+            v_codes[:].bitcast(U16), picked_words[:].bitcast(U16).rearrange("p (j d) -> p d j", d=2)
+        )
+        v_planes = []
+        for a in range(2):
+            plane = keep.tile([P, J], U8, name="v_plane%d" % a, align_bytes=64)
+            nc.vector.tensor_copy(plane[:], table_planes[:, a, :].indirect(offsets[:]))
+            v_planes.append(plane)
+
+        def quantise(name, raw):
+            width = raw.shape[2]
+            grouped = ring.tile([P, width, PACK], BF16, name="grouped", align_bytes=64, bufs=2)
+            nc.scalar.copy(
+                grouped[:].rearrange("p (c s) i -> p c i s", s=4), raw[:].rearrange("p i (c s) -> p c i s", s=4)
+            )
+            codes = keep.tile([P, width], U32, name=name + "_codes", align_bytes=64)
+            plane = keep.tile([P, width], U8, name=name + "_plane", align_bytes=64)
+            nc.vector.quantize_mx(codes[:].bitcast(FP8X4), plane[:], grouped[:].rearrange("p c i -> p (c i)"))
+            return codes, plane
+
+        x_q = [quantise("x0", x_raw[0])]
+        wz_q = [quantise("wz0", wz_raw[0])]
+        wn_q = [quantise("wn0", wn_raw[0])]
+        x_q.append(quantise("x1", x_raw[1]))
+
+        def message_pass(bank, w_q, c, h, stop):
+            codes, plane = w_q[c * P // W_PIECE]
+            cols = slice(c * P % W_PIECE, c * P % W_PIECE + P)
+            nc.tensor.matmul_mx(
+                bank[:], codes[:, cols].bitcast(FP8X4), plane[:, cols],
+                x_q[h][0][:].bitcast(FP8X4), x_q[h][1][:], start=True, stop=stop,
+            )
+
+        def state_passes(bank, u_codes, u_planes, c, h, start):
+            for a in range(2):
+                nc.tensor.matmul_mx(
+                    bank[:],
+                    u_codes[:, a, 2 * c * P : 2 * (c + 1) * P].bitcast(FP4X4),
+                    u_planes[:, a, c * P : (c + 1) * P],
+                    v_codes[:, a, 2 * h * HALF : 2 * (h + 1) * HALF].bitcast(FP4X4),
+                    v_planes[a][:, h * HALF : (h + 1) * HALF],
+                    start=start and a == 0, stop=a == 1,
+                )
+
+        def candidate(c):
+            gate = ring.tile([P, J], F32, name="gate", bufs=2)
+            rest = ring.tile([P, J], F32, name="rest", bufs=3)
+            cand = ring.tile([P, J], F32, name="cand", bufs=2)
+            xn_banks = []
+            for h in range(2):
+                cols = slice(h * HALF, (h + 1) * HALF)
+                sz = psum.tile([P, HALF], F32, name="sz", bufs=2)
+                message_pass(sz, wz_q, c, h, False)
+                state_passes(sz, uz_codes, uz_planes, c, h, False)
+                nc.scalar.activation(gate[:, cols], sz[:], ACT.Sigmoid, bias=bz_cols[:, c : c + 1])
+                nc.scalar.activation(rest[:, cols], sz[:], ACT.Sigmoid, bias=bz_negated[:, c : c + 1], scale=-1.0)
+                hn = psum.tile([P, HALF], F32, name="hn", bufs=3)
+                state_passes(hn, un_codes, un_planes, c, h, True)
+                xn = psum.tile([P, HALF], F32, name="xn", bufs=3)
+                message_pass(xn, wn_q, c, h, True)
+                nc.vector.tensor_tensor(cand[:, cols], hn[:], gate[:, cols], ALU.mult)
+                xn_banks.append(xn)
+            for h in range(2):
+                cols = slice(h * HALF, (h + 1) * HALF)
+                nc.vector.tensor_tensor(cand[:, cols], xn_banks[h][:], cand[:, cols], ALU.add)
+            nc.scalar.activation(cand[:], cand[:], ACT.Tanh, bias=bn_cols[:, c : c + 1])
+            return cand, rest
+
+        def blend(c, cand, rest):
+            engine = nc.vector if c == 0 else nc.gpsimd
+            diff = ring.tile([P, J], F32, name="diff", bufs=1)
+            result = ring.tile([P, J], F32, name="result", bufs=2)
+            nc.vector.tensor_tensor(diff[:], states[c][:].indirect(offsets[:]), cand[:], ALU.subtract)
+            spans = halves if c == CHUNKS - 1 else [slice(0, J)]
+            for cols in spans:
+                engine.tensor_tensor(diff[:, cols], diff[:, cols], rest[:, cols], ALU.mult)
+                engine.tensor_tensor(result[:, cols], diff[:, cols], cand[:, cols], ALU.add)
+                engine.tensor_tensor(result[:, cols], result[:, cols], weight[:, cols], ALU.mult)
+            return result, spans
+
+        def put(c, result, spans):
+            page = pages[c % 2]
+            for cols in spans:
+                nc.vector.tensor_copy(page[:].indirect(offsets[:, cols.start // 16 : cols.stop // 16]), result[:, cols])
+            nc.sync.dma_start(out[c * P : (c + 1) * P, :], page[:])
+
+        halves = [slice(0, HALF), slice(HALF, J)]
+        made = [candidate(0), candidate(1)]
+        blended = [blend(0, *made[0])]
+        for c in range(CHUNKS):
+            i = c // 2 + 1
+            if c % 2 == 0 and i < N // W_PIECE:
+                wz_q.append(quantise("wz%d" % i, wz_raw[i]))
+                wn_q.append(quantise("wn%d" % i, wn_raw[i]))
+            if c + 2 < CHUNKS:
+                made.append(candidate(c + 2))
+            if c + 1 < CHUNKS:
+                blended.append(blend(c + 1, *made[c + 1]))
+            put(c, *blended[c])

@@ -21,7 +21,7 @@ PACK = 4
 HALF = 512
 W_PIECE = 256
 CHUNKS = N // P
-AHEAD = 2
+LATE = 128
 
 
 def tile_list_tgn_mgu_kernel(
@@ -71,13 +71,19 @@ def tile_list_tgn_mgu_kernel(
             nc.sync.dma_start(tile[:].bitcast(I32), words.bitcast(I32).rearrange("a p n -> p a n"))
             return tile
 
-        def load_state(c):
-            rows = keep.tile([P, T], F32, name="state%d" % c)
+        def load_state(c, tag=None):
+            rows = keep.tile([P, T], F32, name="state%d" % c, tag=tag or "state%d" % c)
             nc.sync.dma_start(rows[:], hT[c * P : (c + 1) * P, :])
             return rows
 
         def piece(i):
             return slice(i * W_PIECE, (i + 1) * W_PIECE)
+
+        def load_gate_bias(c):
+            col = keep.tile([P, 1], F32, name="bz%d" % c)
+            with nc.allow_non_contiguous_dma(reason="one bias value a partition"):
+                nc.sync.dma_start(col[:], bz[c * P : (c + 1) * P].rearrange("(p o) -> p o", o=1))
+            return col
 
         x_raw = [load_rows("x_raw0", x, slice(0, HALF))]
         wz_raw = [load_rows("wz_raw0", wz, piece(0))]
@@ -87,22 +93,23 @@ def tile_list_tgn_mgu_kernel(
         un_codes = load_words("un_codes", un_words)
         x_raw.append(load_rows("x_raw1", x, slice(HALF, J)))
         load_scale_rows(un_planes, un_scales)
-        bz_cols = keep.tile([P, CHUNKS], F32, name="bz_cols")
+        bz_cols = [load_gate_bias(0)]
         bn_cols = keep.tile([P, CHUNKS], F32, name="bn_cols")
         with nc.allow_non_contiguous_dma(reason="one bias value a partition"):
-            nc.sync.dma_start(bz_cols[:], bz.rearrange("(c p) -> p c", p=P))
             nc.sync.dma_start(bn_cols[:], bn.rearrange("(c p) -> p c", p=P))
-        bz_negated = keep.tile([P, CHUNKS], F32, name="bz_negated")
-        nc.scalar.activation(bz_negated[:], bz_cols[:], ACT.Copy, scale=-1.0)
-        states = [load_state(0)]
         weight = keep.tile([P, J], F32, name="weight")
-        nc.sync.dma_start(weight[:], wgo)
-        states.append(load_state(1))
-        for i in range(1, N // W_PIECE):
-            wz_raw.append(load_rows("wz_raw%d" % i, wz, piece(i)))
-            wn_raw.append(load_rows("wn_raw%d" % i, wn, piece(i)))
-            states.append(load_state(2 * i))
-            states.append(load_state(2 * i + 1))
+        states = []
+        for c in range(CHUNKS - 1):
+            i = c // 2 + 1
+            if c % 2 == 0 and i < N // W_PIECE:
+                wz_raw.append(load_rows("wz_raw%d" % i, wz, piece(i)))
+                wn_raw.append(load_rows("wn_raw%d" % i, wn, piece(i)))
+            states.append(load_state(c))
+            if c == CHUNKS - 2:
+                states.append(load_state(c + 1))
+            bz_cols.append(load_gate_bias(c + 1))
+            if c == 0:
+                nc.sync.dma_start(weight[:], wgo)
 
         picked_words = keep.tile([P, J], U32, name="picked_words")
         nc.vector.tensor_copy(picked_words[:], table_words[:].indirect(offsets[:]))
@@ -151,58 +158,90 @@ def tile_list_tgn_mgu_kernel(
                     start=start and a == 0, stop=a == 1,
                 )
 
+        halves = [slice(0, HALF), slice(HALF, J)]
+        stage = keep.tile([P, 2 * J], F32, name="stage")
+
+        def region(c):
+            return stage[:, c % 2 * J : (c % 2 + 1) * J]
+
+        def late_cols(c):
+            return slice(0, LATE) if c % 2 else slice(J - LATE, J)
+
+        def early_cols(c):
+            return slice(LATE, J) if c % 2 else slice(0, J - LATE)
+
+        def scratch(c, h):
+            if h == 0:
+                start = J + LATE - HALF if c % 2 else J - LATE
+            else:
+                start = 0 if c % 2 else 2 * J - HALF
+            return stage[:, start : start + HALF]
+
         def candidate(c):
             gate = ring.tile([P, J], F32, name="gate", bufs=2)
             rest = ring.tile([P, J], F32, name="rest", bufs=3)
-            cand = ring.tile([P, J], F32, name="cand", bufs=2)
+            cand = ring.tile([P, J], F32, name="cand", bufs=3)
             xn_banks = []
-            for h in range(2):
-                cols = slice(h * HALF, (h + 1) * HALF)
+            for h, cols in enumerate(halves):
                 sz = psum.tile([P, HALF], F32, name="sz", bufs=2)
                 message_pass(sz, wz_q, c, h, False)
                 state_passes(sz, uz_codes, uz_planes, c, h, False)
-                nc.scalar.activation(gate[:, cols], sz[:], ACT.Sigmoid, bias=bz_cols[:, c : c + 1])
-                nc.scalar.activation(rest[:, cols], sz[:], ACT.Sigmoid, bias=bz_negated[:, c : c + 1], scale=-1.0)
+                nc.scalar.activation(gate[:, cols], sz[:], ACT.Sigmoid, bias=bz_cols[c][:])
                 hn = psum.tile([P, HALF], F32, name="hn", bufs=3)
                 state_passes(hn, un_codes, un_planes, c, h, True)
                 xn = psum.tile([P, HALF], F32, name="xn", bufs=3)
                 message_pass(xn, wn_q, c, h, True)
-                nc.vector.tensor_tensor(cand[:, cols], hn[:], gate[:, cols], ALU.mult)
+                nc.vector.tensor_tensor(scratch(c, h), hn[:], gate[:, cols], ALU.mult)
                 xn_banks.append(xn)
-            for h in range(2):
-                cols = slice(h * HALF, (h + 1) * HALF)
-                nc.vector.tensor_tensor(cand[:, cols], xn_banks[h][:], cand[:, cols], ALU.add)
+            nc.scalar.activation(rest[:], gate[:], ACT.Copy, bias=1.0, scale=-1.0)
+            for h, cols in enumerate(halves):
+                nc.vector.tensor_tensor(cand[:, cols], xn_banks[h][:], scratch(c, h), ALU.add)
             nc.scalar.activation(cand[:], cand[:], ACT.Tanh, bias=bn_cols[:, c : c + 1])
-            return cand, rest
+            return gate, rest, cand
 
-        def blend(c, cand, rest):
+        def look_up(c, kept):
+            nc.vector.tensor_tensor(kept, states[c][:].indirect(offsets[:]), made[c][1][:], ALU.mult)
+
+        def gated(c):
+            gate, rest, cand = made[c]
+            engine = nc.vector if c < 2 else nc.gpsimd
+            engine.tensor_tensor(cand[:], cand[:], gate[:], ALU.mult)
+
+        def join(c, kept):
             engine = nc.vector if c == 0 else nc.gpsimd
-            diff = ring.tile([P, J], F32, name="diff", bufs=1)
-            result = ring.tile([P, J], F32, name="result", bufs=2)
-            nc.vector.tensor_tensor(diff[:], states[c][:].indirect(offsets[:]), cand[:], ALU.subtract)
-            spans = halves if c == CHUNKS - 1 else [slice(0, J)]
-            for cols in spans:
-                engine.tensor_tensor(diff[:, cols], diff[:, cols], rest[:, cols], ALU.mult)
-                engine.tensor_tensor(result[:, cols], diff[:, cols], cand[:, cols], ALU.add)
-                engine.tensor_tensor(result[:, cols], result[:, cols], weight[:, cols], ALU.mult)
-            return result, spans
+            engine.tensor_tensor(made[c][2][:], made[c][2][:], kept, ALU.add)
 
-        def put(c, result, spans):
-            page = pages[c % 2]
-            for cols in spans:
-                nc.vector.tensor_copy(page[:].indirect(offsets[:, cols.start // 16 : cols.stop // 16]), result[:, cols])
-            nc.sync.dma_start(out[c * P : (c + 1) * P, :], page[:])
+        def weigh(c, cols):
+            engine = nc.vector if c == 0 else nc.gpsimd
+            engine.tensor_tensor(region(c)[:, cols], made[c][2][:, cols], weight[:, cols], ALU.mult)
 
-        halves = [slice(0, HALF), slice(HALF, J)]
-        made = [candidate(0), candidate(1)]
-        blended = [blend(0, *made[0])]
-        for c in range(CHUNKS):
-            i = c // 2 + 1
-            if c % 2 == 0 and i < N // W_PIECE:
+        made = []
+        for c in range(-2, CHUNKS):
+            i = (c + 3) // 2
+            if c % 2 == 1 and i < N // W_PIECE:
                 wz_q.append(quantise("wz%d" % i, wz_raw[i]))
                 wn_q.append(quantise("wn%d" % i, wn_raw[i]))
             if c + 2 < CHUNKS:
+                if c >= 0:
+                    weigh(c, early_cols(c))
                 made.append(candidate(c + 2))
-            if c + 1 < CHUNKS:
-                blended.append(blend(c + 1, *made[c + 1]))
-            put(c, *blended[c])
+                if c >= 0:
+                    weigh(c, late_cols(c))
+            else:
+                weigh(c, slice(0, J))
+            if 0 <= c + 1 < CHUNKS - 1:
+                kept = region(c + 1)
+                look_up(c + 1, kept)
+            if c + 2 == CHUNKS - 1:
+                last_kept = made[c + 1][1][:]
+                look_up(c + 2, last_kept)
+            if c + 1 in (0, 1):
+                gated(c + 1)
+            if 0 <= c + 1 < CHUNKS:
+                join(c + 1, kept if c + 1 < CHUNKS - 1 else last_kept)
+            if c >= 0:
+                page = pages[c % 2]
+                nc.vector.tensor_copy(page[:].indirect(offsets[:]), region(c))
+                nc.sync.dma_start(out[c * P : (c + 1) * P, :], page[:])
+            if 2 <= c + 2 < CHUNKS:
+                gated(c + 2)

@@ -1,6 +1,7 @@
 from contextlib import ExitStack
 
 import concourse.mybir as mybir
+from concourse.masks import make_identity
 
 K, M, N, T, J = 512, 1024, 1024, 2048, 1024
 FLOPS = 2 * 2 * (K + M) * N * J
@@ -21,7 +22,6 @@ PACK = 4
 HALF = 512
 W_PIECE = 256
 CHUNKS = N // P
-LATE = 128
 
 
 def tile_list_tgn_mgu_kernel(
@@ -43,8 +43,8 @@ def tile_list_tgn_mgu_kernel(
             nc.vector.memset(planes[:].bitcast(I32), 0)
             return planes
 
-        def load_scale_rows(planes, scales):
-            for q in range(4):
+        def load_scale_rows(planes, scales, quadrants):
+            for q in quadrants:
                 nc.sync.dma_start(
                     planes[32 * q : 32 * q + 4].bitcast(I32),
                     scales[:, 4 * q : 4 * q + 4, :].bitcast(I32).rearrange("a r n -> r a n"),
@@ -53,7 +53,12 @@ def tile_list_tgn_mgu_kernel(
         table_planes = cleared_planes("table_planes", T)
         uz_planes = cleared_planes("uz_planes", N)
         un_planes = cleared_planes("un_planes", N)
-        load_scale_rows(table_planes, tab_scales)
+        bias_rows = keep.tile([P, P], F32, name="bias_rows")
+        nc.vector.memset(bias_rows[:], 0.0)
+        identity = keep.tile([P, P], F32, name="identity")
+        make_identity(nc, identity[:])
+        warm = keep.tile([P, 1], F32, name="warm")
+        nc.scalar.activation(warm[:], identity[:, 0:1], ACT.Sigmoid)
 
         pages = []
         for b in range(2):
@@ -79,72 +84,76 @@ def tile_list_tgn_mgu_kernel(
         def piece(i):
             return slice(i * W_PIECE, (i + 1) * W_PIECE)
 
-        def load_gate_bias(c):
-            col = keep.tile([P, 1], F32, name="bz%d" % c)
-            with nc.allow_non_contiguous_dma(reason="one bias value a partition"):
-                nc.sync.dma_start(col[:], bz[c * P : (c + 1) * P].rearrange("(p o) -> p o", o=1))
-            return col
-
+        load_scale_rows(table_planes, tab_scales, (0, 1))
         x_raw = [load_rows("x_raw0", x, slice(0, HALF))]
+        load_scale_rows(table_planes, tab_scales, (2, 3))
         wz_raw = [load_rows("wz_raw0", wz, piece(0))]
-        load_scale_rows(uz_planes, uz_scales)
+        load_scale_rows(uz_planes, uz_scales, (0, 1))
         uz_codes = load_words("uz_codes", uz_words)
-        wn_raw = [load_rows("wn_raw0", wn, piece(0))]
-        un_codes = load_words("un_codes", un_words)
+        load_scale_rows(uz_planes, uz_scales, (2, 3))
         x_raw.append(load_rows("x_raw1", x, slice(HALF, J)))
-        load_scale_rows(un_planes, un_scales)
-        bz_cols = [load_gate_bias(0)]
-        bn_cols = keep.tile([P, CHUNKS], F32, name="bn_cols")
-        with nc.allow_non_contiguous_dma(reason="one bias value a partition"):
-            nc.sync.dma_start(bn_cols[:], bn.rearrange("(c p) -> p c", p=P))
+        nc.sync.dma_start(bias_rows[0:CHUNKS, :], bz.rearrange("(c p) -> c p", p=P))
+        nc.sync.dma_start(bias_rows[CHUNKS : 2 * CHUNKS, :], bn.rearrange("(c p) -> c p", p=P))
+        un_codes = load_words("un_codes", un_words)
+        load_scale_rows(un_planes, un_scales, (0, 1))
+        wn_raw = [load_rows("wn_raw0", wn, piece(0))]
+        load_scale_rows(un_planes, un_scales, (2, 3))
         weight = keep.tile([P, J], F32, name="weight")
         states = []
-        for c in range(CHUNKS - 1):
+        for c in range(CHUNKS):
+            states.append(load_state(c))
             i = c // 2 + 1
             if c % 2 == 0 and i < N // W_PIECE:
                 wz_raw.append(load_rows("wz_raw%d" % i, wz, piece(i)))
                 wn_raw.append(load_rows("wn_raw%d" % i, wn, piece(i)))
-            states.append(load_state(c))
-            if c == CHUNKS - 2:
-                states.append(load_state(c + 1))
-            bz_cols.append(load_gate_bias(c + 1))
             if c == 0:
                 nc.sync.dma_start(weight[:], wgo)
 
-        picked_words = keep.tile([P, J], U32, name="picked_words")
-        nc.vector.tensor_copy(picked_words[:], table_words[:].indirect(offsets[:]))
-        v_codes = keep.tile([P, 2, 2 * J], U8, name="v_codes", align_bytes=64)
-        nc.vector.tensor_copy(
-            v_codes[:].bitcast(U16), picked_words[:].bitcast(U16).rearrange("p (j d) -> p d j", d=2)
-        )
-        v_planes = []
-        for a in range(2):
-            plane = keep.tile([P, J], U8, name="v_plane%d" % a, align_bytes=64)
-            nc.vector.tensor_copy(plane[:], table_planes[:, a, :].indirect(offsets[:]))
-            v_planes.append(plane)
+        bias_bank = psum.tile([P, P], F32, name="bias_bank", tag="xn", bufs=3)
+        nc.tensor.transpose(bias_bank[:], bias_rows[:], identity[:])
+        bias_cols = keep.tile([P, 2 * CHUNKS], F32, name="bias_cols")
+        nc.scalar.copy(bias_cols[:], bias_bank[:, : 2 * CHUNKS])
 
-        def quantise(name, raw):
-            width = raw.shape[2]
-            grouped = ring.tile([P, width, PACK], BF16, name="grouped", align_bytes=64, bufs=2)
-            nc.scalar.copy(
-                grouped[:].rearrange("p (c s) i -> p c i s", s=4), raw[:].rearrange("p i (c s) -> p c i s", s=4)
-            )
-            codes = keep.tile([P, width], U32, name=name + "_codes", align_bytes=64)
-            plane = keep.tile([P, width], U8, name=name + "_plane", align_bytes=64)
-            nc.vector.quantize_mx(codes[:].bitcast(FP8X4), plane[:], grouped[:].rearrange("p c i -> p (c i)"))
-            return codes, plane
+        halves = [slice(0, HALF), slice(HALF, J)]
 
-        x_q = [quantise("x0", x_raw[0])]
-        wz_q = [quantise("wz0", wz_raw[0])]
-        wn_q = [quantise("wn0", wn_raw[0])]
-        x_q.append(quantise("x1", x_raw[1]))
+        def look_up_table(h, tags):
+            part = offsets[:, h * HALF // 16 : (h + 1) * HALF // 16]
+            picked = keep.tile([P, HALF], U32, name="picked%d" % h, tag=tags[2], align_bytes=64)
+            nc.vector.tensor_copy(picked[:], table_words[:].indirect(part))
+            planes = []
+            for a in range(2):
+                plane = keep.tile([P, HALF], U8, name="v_plane%d_%d" % (h, a), tag=tags[a], align_bytes=64)
+                nc.vector.tensor_copy(plane[:], table_planes[:, a, :].indirect(part))
+                planes.append(plane)
+            codes = keep.tile([P, 2, 2 * HALF], U8, name="v_codes%d" % h, align_bytes=64)
+            nc.vector.tensor_copy(codes[:].bitcast(U16), picked[:].bitcast(U16).rearrange("p (j d) -> p d j", d=2))
+            return codes, planes
+
+        def quantise(name, raws, pool, tag):
+            width = raws[0].shape[2]
+            grouped = pool.tile([P, len(raws), width, PACK], BF16, name="grouped_" + name, tag=tag, align_bytes=64, bufs=1)
+            for n, raw in enumerate(raws):
+                nc.scalar.copy(
+                    grouped[:, n].rearrange("p (c s) i -> p c i s", s=4), raw[:].rearrange("p i (c s) -> p c i s", s=4)
+                )
+            codes = keep.tile([P, len(raws) * width], U32, name=name + "_codes", align_bytes=64)
+            plane = keep.tile([P, len(raws) * width], U8, name=name + "_plane", align_bytes=64)
+            nc.vector.quantize_mx(codes[:].bitcast(FP8X4), plane[:], grouped[:].rearrange("p n c i -> p (n c i)"))
+            return [(codes[:, n * width : (n + 1) * width], plane[:, n * width : (n + 1) * width]) for n in range(len(raws))]
+
+        v_q = [look_up_table(0, ["v_plane0", "v_plane1", "picked0"])]
+        x_q = quantise("x0", [x_raw[0]], keep, "grouped_x0")
+        wz_q = quantise("wz0", [wz_raw[0]], keep, "grouped_wz0")
+        v_q.append(look_up_table(1, ["grouped_x0", "grouped_wz0", "picked1"]))
+        x_q.extend(quantise("x1", [x_raw[1]], keep, "grouped_x1"))
+        wn_q = quantise("wn0", [wn_raw[0]], keep, "grouped_wn0")
 
         def message_pass(bank, w_q, c, h, stop):
             codes, plane = w_q[c * P // W_PIECE]
             cols = slice(c * P % W_PIECE, c * P % W_PIECE + P)
             nc.tensor.matmul_mx(
                 bank[:], codes[:, cols].bitcast(FP8X4), plane[:, cols],
-                x_q[h][0][:].bitcast(FP8X4), x_q[h][1][:], start=True, stop=stop,
+                x_q[h][0].bitcast(FP8X4), x_q[h][1], start=True, stop=stop,
             )
 
         def state_passes(bank, u_codes, u_planes, c, h, start):
@@ -153,95 +162,81 @@ def tile_list_tgn_mgu_kernel(
                     bank[:],
                     u_codes[:, a, 2 * c * P : 2 * (c + 1) * P].bitcast(FP4X4),
                     u_planes[:, a, c * P : (c + 1) * P],
-                    v_codes[:, a, 2 * h * HALF : 2 * (h + 1) * HALF].bitcast(FP4X4),
-                    v_planes[a][:, h * HALF : (h + 1) * HALF],
+                    v_q[h][0][:, a, :].bitcast(FP4X4),
+                    v_q[h][1][a][:],
                     start=start and a == 0, stop=a == 1,
                 )
 
-        halves = [slice(0, HALF), slice(HALF, J)]
-        stage = keep.tile([P, 2 * J], F32, name="stage")
-
-        def region(c):
-            return stage[:, c % 2 * J : (c % 2 + 1) * J]
-
-        def late_cols(c):
-            return slice(0, LATE) if c % 2 else slice(J - LATE, J)
-
-        def early_cols(c):
-            return slice(LATE, J) if c % 2 else slice(0, J - LATE)
-
-        def scratch(c, h):
-            if h == 0:
-                start = J + LATE - HALF if c % 2 else J - LATE
+        def products(c):
+            if c == 0:
+                gate = ring.tile([P, J], F32, name="gate0", tag="first", align_bytes=64, bufs=1)
             else:
-                start = 0 if c % 2 else 2 * J - HALF
-            return stage[:, start : start + HALF]
-
-        def candidate(c):
-            gate = ring.tile([P, J], F32, name="gate", bufs=2)
-            rest = ring.tile([P, J], F32, name="rest", bufs=3)
-            cand = ring.tile([P, J], F32, name="cand", bufs=3)
-            xn_banks = []
+                gate = ring.tile([P, J], F32, name="gate", bufs=2)
+            rest = ring.tile([P, J], F32, name="rest", bufs=2)
+            cand = ring.tile([P, J], F32, name="cand", bufs=2)
+            hn_banks, xn_banks = [], []
             for h, cols in enumerate(halves):
                 sz = psum.tile([P, HALF], F32, name="sz", bufs=2)
                 message_pass(sz, wz_q, c, h, False)
                 state_passes(sz, uz_codes, uz_planes, c, h, False)
-                nc.scalar.activation(gate[:, cols], sz[:], ACT.Sigmoid, bias=bz_cols[c][:])
+                nc.scalar.activation(gate[:, cols], sz[:], ACT.Sigmoid, bias=bias_cols[:, c : c + 1])
                 hn = psum.tile([P, HALF], F32, name="hn", bufs=3)
                 state_passes(hn, un_codes, un_planes, c, h, True)
                 xn = psum.tile([P, HALF], F32, name="xn", bufs=3)
                 message_pass(xn, wn_q, c, h, True)
-                nc.vector.tensor_tensor(scratch(c, h), hn[:], gate[:, cols], ALU.mult)
+                hn_banks.append(hn)
                 xn_banks.append(xn)
-            nc.scalar.activation(rest[:], gate[:], ACT.Copy, bias=1.0, scale=-1.0)
-            for h, cols in enumerate(halves):
-                nc.vector.tensor_tensor(cand[:, cols], xn_banks[h][:], scratch(c, h), ALU.add)
-            nc.scalar.activation(cand[:], cand[:], ACT.Tanh, bias=bn_cols[:, c : c + 1])
-            return gate, rest, cand
+            return gate, rest, cand, hn_banks, xn_banks
 
-        def look_up(c, kept):
-            nc.vector.tensor_tensor(kept, states[c][:].indirect(offsets[:]), made[c][1][:], ALU.mult)
+        def gate_state_part(step, h):
+            gate, rest, cand, hn_banks, xn_banks = step
+            nc.vector.tensor_tensor(cand[:, halves[h]], hn_banks[h][:], gate[:, halves[h]], ALU.mult)
 
-        def gated(c):
-            gate, rest, cand = made[c]
-            engine = nc.vector if c < 2 else nc.gpsimd
-            engine.tensor_tensor(cand[:], cand[:], gate[:], ALU.mult)
+        def add_message_part(step, h):
+            gate, rest, cand, hn_banks, xn_banks = step
+            nc.vector.tensor_tensor(cand[:, halves[h]], xn_banks[h][:], cand[:, halves[h]], ALU.add)
 
-        def join(c, kept):
-            engine = nc.vector if c == 0 else nc.gpsimd
-            engine.tensor_tensor(made[c][2][:], made[c][2][:], kept, ALU.add)
+        def squash(step, c):
+            nc.scalar.activation(step[2][:], step[2][:], ACT.Tanh, bias=bias_cols[:, CHUNKS + c : CHUNKS + c + 1])
 
-        def weigh(c, cols):
-            engine = nc.vector if c == 0 else nc.gpsimd
-            engine.tensor_tensor(region(c)[:, cols], made[c][2][:, cols], weight[:, cols], ALU.mult)
+        def complement(step):
+            nc.scalar.activation(step[1][:], step[0][:], ACT.Copy, bias=1.0, scale=-1.0)
 
-        made = []
-        for c in range(-2, CHUNKS):
-            i = (c + 3) // 2
-            if c % 2 == 1 and i < N // W_PIECE:
-                wz_q.append(quantise("wz%d" % i, wz_raw[i]))
-                wn_q.append(quantise("wn%d" % i, wn_raw[i]))
-            if c + 2 < CHUNKS:
-                if c >= 0:
-                    weigh(c, early_cols(c))
-                made.append(candidate(c + 2))
-                if c >= 0:
-                    weigh(c, late_cols(c))
-            else:
-                weigh(c, slice(0, J))
-            if 0 <= c + 1 < CHUNKS - 1:
-                kept = region(c + 1)
-                look_up(c + 1, kept)
-            if c + 2 == CHUNKS - 1:
-                last_kept = made[c + 1][1][:]
-                look_up(c + 2, last_kept)
-            if c + 1 in (0, 1):
-                gated(c + 1)
-            if 0 <= c + 1 < CHUNKS:
-                join(c + 1, kept if c + 1 < CHUNKS - 1 else last_kept)
-            if c >= 0:
-                page = pages[c % 2]
-                nc.vector.tensor_copy(page[:].indirect(offsets[:]), region(c))
-                nc.sync.dma_start(out[c * P : (c + 1) * P, :], page[:])
-            if 2 <= c + 2 < CHUNKS:
-                gated(c + 2)
+        def quantise_weights(i, tag):
+            pair = quantise("w%d" % i, [wz_raw[i], wn_raw[i]], ring, tag)
+            wz_q.append(pair[0])
+            wn_q.append(pair[1])
+
+        step = products(0)
+        for h in range(2):
+            gate_state_part(step, h)
+        for h in range(2):
+            add_message_part(step, h)
+        squash(step, 0)
+        complement(step)
+        for c in range(CHUNKS):
+            gate, rest, cand = step[:3]
+            more = c + 1 < CHUNKS
+            if c in (2, 4):
+                quantise_weights(c // 2 + 1, "diff")
+            if more:
+                step = products(c + 1)
+                complement(step)
+            if c == 0:
+                quantise_weights(1, "first")
+            diff = ring.tile([P, J], F32, name="diff", align_bytes=64, bufs=1)
+            nc.vector.tensor_tensor(diff[:], states[c][:].indirect(offsets[:]), cand[:], ALU.subtract)
+            if more:
+                gate_state_part(step, 0)
+            nc.vector.tensor_tensor(diff[:], diff[:], rest[:], ALU.mult)
+            if more:
+                gate_state_part(step, 1)
+                add_message_part(step, 0)
+            blend = step[0] if c > 0 else ring.tile([P, J], F32, name="blend0", tag="first", align_bytes=64, bufs=1)
+            nc.vector.tensor_tensor(blend[:], diff[:], cand[:], ALU.add)
+            if more:
+                add_message_part(step, 1)
+                squash(step, c + 1)
+            page = pages[c % 2]
+            nc.vector.tensor_tensor(page[:].indirect(offsets[:]), blend[:], weight[:], ALU.mult)
+            nc.scalar.dma_start(out[c * P : (c + 1) * P, :], page[:])

@@ -19,9 +19,12 @@ ACT = mybir.ActivationFunctionType
 
 P = 128
 PACK = 4
+STATE_PASSES = M // (P * PACK)
 HALF = 512
-W_PIECE = 256
 CHUNKS = N // P
+PIECE = 256
+TABLE_LOADS = 4
+LIST_ROWS = 16
 
 
 def tile_list_tgn_mgu_kernel(
@@ -30,25 +33,13 @@ def tile_list_tgn_mgu_kernel(
     nc = tc.nc
     with ExitStack() as ctx:
         keep = ctx.enter_context(tc.tile_pool(name="keep", bufs=1))
-        ring = ctx.enter_context(tc.tile_pool(name="ring", bufs=3))
+        ring = ctx.enter_context(tc.tile_pool(name="ring", bufs=2))
         psum = ctx.enter_context(tc.psum_pool(name="psum", bufs=1))
 
-        offsets = keep.tile([P, J // 16], U16, name="offsets")
-        nc.sync.dma_start(offsets[:], offs)
-        table_words = keep.tile([P, T], U32, name="table_words")
-        nc.sync.dma_start(table_words[:].bitcast(I32), tab_words[0].rearrange("p t b -> p (t b)").bitcast(I32))
-
         def cleared_planes(name, width):
-            planes = keep.tile([P, 2, width], U8, name=name, align_bytes=64)
+            planes = keep.tile([P, STATE_PASSES, width], U8, name=name, align_bytes=64)
             nc.vector.memset(planes[:].bitcast(I32), 0)
             return planes
-
-        def load_scale_rows(planes, scales, quadrants):
-            for q in quadrants:
-                nc.sync.dma_start(
-                    planes[32 * q : 32 * q + 4].bitcast(I32),
-                    scales[:, 4 * q : 4 * q + 4, :].bitcast(I32).rearrange("a r n -> r a n"),
-                )
 
         table_planes = cleared_planes("table_planes", T)
         uz_planes = cleared_planes("uz_planes", N)
@@ -57,8 +48,6 @@ def tile_list_tgn_mgu_kernel(
         nc.vector.memset(bias_rows[:], 0.0)
         identity = keep.tile([P, P], F32, name="identity")
         make_identity(nc, identity[:])
-        warm = keep.tile([P, 1], F32, name="warm")
-        nc.scalar.activation(warm[:], identity[:, 0:1], ACT.Sigmoid)
 
         pages = []
         for b in range(2):
@@ -66,46 +55,51 @@ def tile_list_tgn_mgu_kernel(
             nc.gpsimd.memset(page[:], 0.0)
             pages.append(page)
 
-        def load_rows(name, src, cols):
-            raw = keep.tile([P, PACK, cols.stop - cols.start], F32, name=name)
-            nc.sync.dma_start(raw[:], src[:, cols].rearrange("(p i) c -> p i c", i=PACK))
+        def load_scale_rows(planes, scales):
+            for q in range(4):
+                nc.sync.dma_start(
+                    planes[32 * q : 32 * q + 4].bitcast(I32),
+                    scales[:, 4 * q : 4 * q + 4, :].bitcast(I32).rearrange("a r n -> r a n"),
+                )
+
+        def load_rows(name, src, start, width):
+            raw = keep.tile([P, PACK, width], F32, name=name)
+            nc.sync.dma_start(raw[:], src[:, start : start + width].rearrange("(p i) c -> p i c", i=PACK))
             return raw
 
         def load_words(name, words):
-            tile = keep.tile([P, 2, 2 * N], U8, name=name, align_bytes=64)
-            nc.sync.dma_start(tile[:].bitcast(I32), words.bitcast(I32).rearrange("a p n -> p a n"))
-            return tile
+            codes = keep.tile([P, STATE_PASSES, 2 * N], U8, name=name, align_bytes=64)
+            nc.sync.dma_start(codes[:].bitcast(I32), words.bitcast(I32).rearrange("a p n -> p a n"))
+            return codes
 
-        def load_state(c, tag=None):
-            rows = keep.tile([P, T], F32, name="state%d" % c, tag=tag or "state%d" % c)
-            nc.sync.dma_start(rows[:], hT[c * P : (c + 1) * P, :])
-            return rows
-
-        def piece(i):
-            return slice(i * W_PIECE, (i + 1) * W_PIECE)
-
-        load_scale_rows(table_planes, tab_scales, (0, 1))
-        x_raw = [load_rows("x_raw0", x, slice(0, HALF))]
-        load_scale_rows(table_planes, tab_scales, (2, 3))
-        wz_raw = [load_rows("wz_raw0", wz, piece(0))]
-        load_scale_rows(uz_planes, uz_scales, (0, 1))
+        offsets = keep.tile([P, J // LIST_ROWS], U16, name="offsets")
+        nc.sync.dma_start(offsets[:], offs)
+        table_words = keep.tile([P, T], U32, name="table_words")
+        words_in_hbm = tab_words[0].rearrange("p t b -> p (t b)").bitcast(I32)
+        for n in range(TABLE_LOADS):
+            cols = slice(n * T // TABLE_LOADS, (n + 1) * T // TABLE_LOADS)
+            nc.sync.dma_start(table_words[:, cols].bitcast(I32), words_in_hbm[:, cols])
+        load_scale_rows(table_planes, tab_scales)
+        x_first = [load_rows("x_first%d" % n, x, n * PIECE, PIECE) for n in range(HALF // PIECE)]
+        wz_raw = [load_rows("wz_raw0", wz, 0, PIECE)]
         uz_codes = load_words("uz_codes", uz_words)
-        load_scale_rows(uz_planes, uz_scales, (2, 3))
-        x_raw.append(load_rows("x_raw1", x, slice(HALF, J)))
+        load_scale_rows(uz_planes, uz_scales)
         nc.sync.dma_start(bias_rows[0:CHUNKS, :], bz.rearrange("(c p) -> c p", p=P))
         nc.sync.dma_start(bias_rows[CHUNKS : 2 * CHUNKS, :], bn.rearrange("(c p) -> c p", p=P))
+        x_second = load_rows("x_second", x, HALF, HALF)
         un_codes = load_words("un_codes", un_words)
-        load_scale_rows(un_planes, un_scales, (0, 1))
-        wn_raw = [load_rows("wn_raw0", wn, piece(0))]
-        load_scale_rows(un_planes, un_scales, (2, 3))
+        load_scale_rows(un_planes, un_scales)
+        wn_raw = [load_rows("wn_raw0", wn, 0, PIECE)]
         weight = keep.tile([P, J], F32, name="weight")
         states = []
         for c in range(CHUNKS):
-            states.append(load_state(c))
+            state = keep.tile([P, T], F32, name="state%d" % c)
+            nc.sync.dma_start(state[:], hT[c * P : (c + 1) * P, :])
+            states.append(state)
             i = c // 2 + 1
-            if c % 2 == 0 and i < N // W_PIECE:
-                wz_raw.append(load_rows("wz_raw%d" % i, wz, piece(i)))
-                wn_raw.append(load_rows("wn_raw%d" % i, wn, piece(i)))
+            if c % 2 == 0 and i < N // PIECE:
+                wz_raw.append(load_rows("wz_raw%d" % i, wz, i * PIECE, PIECE))
+                wn_raw.append(load_rows("wn_raw%d" % i, wn, i * PIECE, PIECE))
             if c == 0:
                 nc.sync.dma_start(weight[:], wgo)
 
@@ -116,22 +110,26 @@ def tile_list_tgn_mgu_kernel(
 
         halves = [slice(0, HALF), slice(HALF, J)]
 
-        def look_up_table(h, tags):
-            part = offsets[:, h * HALF // 16 : (h + 1) * HALF // 16]
-            picked = keep.tile([P, HALF], U32, name="picked%d" % h, tag=tags[2], align_bytes=64)
+        def look_up_table(h, plane_tags):
+            part = offsets[:, h * HALF // LIST_ROWS : (h + 1) * HALF // LIST_ROWS]
+            picked = keep.tile([P, HALF], U32, name="picked%d" % h)
             nc.vector.tensor_copy(picked[:], table_words[:].indirect(part))
             planes = []
-            for a in range(2):
-                plane = keep.tile([P, HALF], U8, name="v_plane%d_%d" % (h, a), tag=tags[a], align_bytes=64)
+            for a in range(STATE_PASSES):
+                plane = keep.tile([P, HALF], U8, name="v_plane%d_%d" % (h, a), tag=plane_tags[a], align_bytes=64)
                 nc.vector.tensor_copy(plane[:], table_planes[:, a, :].indirect(part))
                 planes.append(plane)
-            codes = keep.tile([P, 2, 2 * HALF], U8, name="v_codes%d" % h, align_bytes=64)
-            nc.vector.tensor_copy(codes[:].bitcast(U16), picked[:].bitcast(U16).rearrange("p (j d) -> p d j", d=2))
+            codes = keep.tile([P, STATE_PASSES, 2 * HALF], U8, name="v_codes%d" % h, align_bytes=64)
+            nc.vector.tensor_copy(
+                codes[:].bitcast(U16), picked[:].bitcast(U16).rearrange("p (j a) -> p a j", a=STATE_PASSES)
+            )
             return codes, planes
 
         def quantise(name, raws, pool, tag):
             width = raws[0].shape[2]
-            grouped = pool.tile([P, len(raws), width, PACK], BF16, name="grouped_" + name, tag=tag, align_bytes=64, bufs=1)
+            grouped = pool.tile(
+                [P, len(raws), width, PACK], BF16, name="grouped_" + name, tag=tag, align_bytes=64, bufs=1
+            )
             for n, raw in enumerate(raws):
                 nc.scalar.copy(
                     grouped[:, n].rearrange("p (c s) i -> p c i s", s=4), raw[:].rearrange("p i (c s) -> p c i s", s=4)
@@ -139,41 +137,49 @@ def tile_list_tgn_mgu_kernel(
             codes = keep.tile([P, len(raws) * width], U32, name=name + "_codes", align_bytes=64)
             plane = keep.tile([P, len(raws) * width], U8, name=name + "_plane", align_bytes=64)
             nc.vector.quantize_mx(codes[:].bitcast(FP8X4), plane[:], grouped[:].rearrange("p n c i -> p (n c i)"))
-            return [(codes[:, n * width : (n + 1) * width], plane[:, n * width : (n + 1) * width]) for n in range(len(raws))]
+            return codes, plane
 
-        v_q = [look_up_table(0, ["v_plane0", "v_plane1", "picked0"])]
-        x_q = quantise("x0", [x_raw[0]], keep, "grouped_x0")
-        wz_q = quantise("wz0", [wz_raw[0]], keep, "grouped_wz0")
-        v_q.append(look_up_table(1, ["grouped_x0", "grouped_wz0", "picked1"]))
-        x_q.extend(quantise("x1", [x_raw[1]], keep, "grouped_x1"))
-        wn_q = quantise("wn0", [wn_raw[0]], keep, "grouped_wn0")
+        v_q = [look_up_table(0, ["v_plane0", "v_plane1"])]
+        x_q = [quantise("x0", x_first, keep, "grouped_x0")]
+        wz_q = [quantise("wz0", [wz_raw[0]], keep, "grouped_wz0") + (0,)]
+        v_q.append(look_up_table(1, ["grouped_x0", "grouped_wz0"]))
+        x_q.append(quantise("x1", [x_second], keep, "grouped_x1"))
+        wn_q = [quantise("wn0", [wn_raw[0]], keep, "grouped_wn0") + (0,)]
+
+        def quantise_weights(i, tag):
+            both = quantise("w%d" % i, [wz_raw[i], wn_raw[i]], ring, tag)
+            wz_q.append(both + (0,))
+            wn_q.append(both + (PIECE,))
 
         def message_pass(bank, w_q, c, h, stop):
-            codes, plane = w_q[c * P // W_PIECE]
-            cols = slice(c * P % W_PIECE, c * P % W_PIECE + P)
+            codes, plane, first = w_q[c * P // PIECE]
+            cols = slice(first + c * P % PIECE, first + c * P % PIECE + P)
+            x_codes, x_plane = x_q[h]
             nc.tensor.matmul_mx(
-                bank[:], codes[:, cols].bitcast(FP8X4), plane[:, cols],
-                x_q[h][0].bitcast(FP8X4), x_q[h][1], start=True, stop=stop,
+                bank[:], codes[:, cols].bitcast(FP8X4), plane[:, cols], x_codes[:].bitcast(FP8X4), x_plane[:],
+                start=True, stop=stop,
             )
 
         def state_passes(bank, u_codes, u_planes, c, h, start):
-            for a in range(2):
+            v_codes, v_planes = v_q[h]
+            for a in range(STATE_PASSES):
                 nc.tensor.matmul_mx(
                     bank[:],
                     u_codes[:, a, 2 * c * P : 2 * (c + 1) * P].bitcast(FP4X4),
                     u_planes[:, a, c * P : (c + 1) * P],
-                    v_q[h][0][:, a, :].bitcast(FP4X4),
-                    v_q[h][1][a][:],
-                    start=start and a == 0, stop=a == 1,
+                    v_codes[:, a, :].bitcast(FP4X4),
+                    v_planes[a][:],
+                    start=start and a == 0,
+                    stop=a == STATE_PASSES - 1,
                 )
 
         def products(c):
             if c == 0:
                 gate = ring.tile([P, J], F32, name="gate0", tag="first", align_bytes=64, bufs=1)
             else:
-                gate = ring.tile([P, J], F32, name="gate", bufs=2)
-            rest = ring.tile([P, J], F32, name="rest", bufs=2)
-            cand = ring.tile([P, J], F32, name="cand", bufs=2)
+                gate = ring.tile([P, J], F32, name="gate")
+            gate_less_one = ring.tile([P, J], F32, name="gate_less_one")
+            cand = ring.tile([P, J], F32, name="cand")
             hn_banks, xn_banks = [], []
             for h, cols in enumerate(halves):
                 sz = psum.tile([P, HALF], F32, name="sz", bufs=2)
@@ -186,57 +192,58 @@ def tile_list_tgn_mgu_kernel(
                 message_pass(xn, wn_q, c, h, True)
                 hn_banks.append(hn)
                 xn_banks.append(xn)
-            return gate, rest, cand, hn_banks, xn_banks
+            return {"gate": gate, "gate_less_one": gate_less_one, "cand": cand, "hn": hn_banks, "xn": xn_banks}
 
-        def gate_state_part(step, h):
-            gate, rest, cand, hn_banks, xn_banks = step
-            nc.vector.tensor_tensor(cand[:, halves[h]], hn_banks[h][:], gate[:, halves[h]], ALU.mult)
+        def lower_gate(chunk):
+            nc.scalar.activation(chunk["gate_less_one"][:], chunk["gate"][:], ACT.Copy, bias=-1.0)
 
-        def add_message_part(step, h):
-            gate, rest, cand, hn_banks, xn_banks = step
-            nc.vector.tensor_tensor(cand[:, halves[h]], xn_banks[h][:], cand[:, halves[h]], ALU.add)
+        def gate_hn(chunk, h):
+            nc.vector.tensor_tensor(chunk["cand"][:, halves[h]], chunk["hn"][h][:], chunk["gate"][:, halves[h]], ALU.mult)
 
-        def squash(step, c):
-            nc.scalar.activation(step[2][:], step[2][:], ACT.Tanh, bias=bias_cols[:, CHUNKS + c : CHUNKS + c + 1])
+        def add_xn(chunk, h):
+            nc.vector.tensor_tensor(chunk["cand"][:, halves[h]], chunk["xn"][h][:], chunk["cand"][:, halves[h]], ALU.add)
 
-        def complement(step):
-            nc.scalar.activation(step[1][:], step[0][:], ACT.Copy, bias=1.0, scale=-1.0)
+        def squash(chunk, c):
+            bias = bias_cols[:, CHUNKS + c : CHUNKS + c + 1]
+            nc.scalar.activation(chunk["cand"][:], chunk["cand"][:], ACT.Tanh, bias=bias)
 
-        def quantise_weights(i, tag):
-            pair = quantise("w%d" % i, [wz_raw[i], wn_raw[i]], ring, tag)
-            wz_q.append(pair[0])
-            wn_q.append(pair[1])
-
-        step = products(0)
+        ahead = products(0)
         for h in range(2):
-            gate_state_part(step, h)
+            gate_hn(ahead, h)
         for h in range(2):
-            add_message_part(step, h)
-        squash(step, 0)
-        complement(step)
+            add_xn(ahead, h)
+        lower_gate(ahead)
+        squash(ahead, 0)
+
         for c in range(CHUNKS):
-            gate, rest, cand = step[:3]
+            gate_less_one, cand = ahead["gate_less_one"], ahead["cand"]
             more = c + 1 < CHUNKS
-            if c in (2, 4):
-                quantise_weights(c // 2 + 1, "diff")
+            next_piece = c // 2 + 1
+            piece_due = c % 2 == 0 and next_piece < N // PIECE
+            if piece_due and c > 0:
+                quantise_weights(next_piece, "kept")
             if more:
-                step = products(c + 1)
-                complement(step)
+                ahead = products(c + 1)
+                lower_gate(ahead)
             if c == 0:
-                quantise_weights(1, "first")
-            diff = ring.tile([P, J], F32, name="diff", align_bytes=64, bufs=1)
-            nc.vector.tensor_tensor(diff[:], states[c][:].indirect(offsets[:]), cand[:], ALU.subtract)
+                quantise_weights(next_piece, "first")
+
+            nc.vector.scalar_tensor_tensor(cand[:], gate_less_one[:], 1.0, cand[:], ALU.add, ALU.mult)
+            kept = ring.tile([P, J], F32, name="kept", align_bytes=64, bufs=1)
+            nc.vector.tensor_tensor(kept[:], states[c][:].indirect(offsets[:]), gate_less_one[:], ALU.mult)
             if more:
-                gate_state_part(step, 0)
-            nc.vector.tensor_tensor(diff[:], diff[:], rest[:], ALU.mult)
+                gate_hn(ahead, 0)
+                gate_hn(ahead, 1)
+                add_xn(ahead, 0)
+            if c == 0:
+                blend = ring.tile([P, J], F32, name="blend0", tag="first", align_bytes=64, bufs=1)
+            else:
+                blend = ahead["gate"]
+            nc.vector.tensor_tensor(blend[:], cand[:], kept[:], ALU.subtract)
             if more:
-                gate_state_part(step, 1)
-                add_message_part(step, 0)
-            blend = step[0] if c > 0 else ring.tile([P, J], F32, name="blend0", tag="first", align_bytes=64, bufs=1)
-            nc.vector.tensor_tensor(blend[:], diff[:], cand[:], ALU.add)
-            if more:
-                add_message_part(step, 1)
-                squash(step, c + 1)
+                add_xn(ahead, 1)
+                squash(ahead, c + 1)
+
             page = pages[c % 2]
             nc.vector.tensor_tensor(page[:].indirect(offsets[:]), blend[:], weight[:], ALU.mult)
             nc.scalar.dma_start(out[c * P : (c + 1) * P, :], page[:])

from contextlib import ExitStack

import concourse.mybir as mybir
from concourse.masks import make_identity

K, M, N, T, J = 512, 1024, 1024, 2048, 1024
FLOPS = 2 * 2 * (K + M) * N * J

F32 = mybir.dt.float32
BF16 = mybir.dt.bfloat16
I32 = mybir.dt.int32
U32 = mybir.dt.uint32
U16 = mybir.dt.uint16
U8 = mybir.dt.uint8
FP8X4 = mybir.dt.float8_e4m3fn_x4
FP4X4 = mybir.dt.float4_e2m1fn_x4
ALU = mybir.AluOpType
ACT = mybir.ActivationFunctionType

P = 128
PACK = 4
STATE_PASSES = M // (P * PACK)
HALF = 512
CHUNKS = N // P
PIECE = 256
TABLE_LOADS = 4
LIST_ROWS = 16


def tile_list_tgn_mgu_kernel(
    tc, x, tab_words, tab_scales, wz, uz_words, uz_scales, wn, un_words, un_scales, bz, bn, hT, wgo, offs, out
):
    nc = tc.nc
    with ExitStack() as ctx:
        keep = ctx.enter_context(tc.tile_pool(name="keep", bufs=1))
        ring = ctx.enter_context(tc.tile_pool(name="ring", bufs=2))
        psum = ctx.enter_context(tc.psum_pool(name="psum", bufs=1))

        def cleared_planes(name, width):
            planes = keep.tile([P, STATE_PASSES, width], U8, name=name, align_bytes=64)
            nc.vector.memset(planes[:].bitcast(I32), 0)
            return planes

        table_planes = cleared_planes("table_planes", T)
        uz_planes = cleared_planes("uz_planes", N)
        un_planes = cleared_planes("un_planes", N)
        bias_rows = keep.tile([P, P], F32, name="bias_rows")
        nc.vector.memset(bias_rows[:], 0.0)
        identity = keep.tile([P, P], F32, name="identity")
        make_identity(nc, identity[:])

        pages = []
        for b in range(2):
            page = keep.tile([P, T], F32, name="page%d" % b)
            nc.gpsimd.memset(page[:], 0.0)
            pages.append(page)

        def load_scale_rows(planes, scales):
            for q in range(4):
                nc.sync.dma_start(
                    planes[32 * q : 32 * q + 4].bitcast(I32),
                    scales[:, 4 * q : 4 * q + 4, :].bitcast(I32).rearrange("a r n -> r a n"),
                )

        def load_rows(name, src, start, width):
            raw = keep.tile([P, PACK, width], F32, name=name)
            nc.sync.dma_start(raw[:], src[:, start : start + width].rearrange("(p i) c -> p i c", i=PACK))
            return raw

        def load_words(name, words):
            codes = keep.tile([P, STATE_PASSES, 2 * N], U8, name=name, align_bytes=64)
            nc.sync.dma_start(codes[:].bitcast(I32), words.bitcast(I32).rearrange("a p n -> p a n"))
            return codes

        offsets = keep.tile([P, J // LIST_ROWS], U16, name="offsets")
        nc.sync.dma_start(offsets[:], offs)
        table_words = keep.tile([P, T], U32, name="table_words")
        words_in_hbm = tab_words[0].rearrange("p t b -> p (t b)").bitcast(I32)
        for n in range(TABLE_LOADS):
            cols = slice(n * T // TABLE_LOADS, (n + 1) * T // TABLE_LOADS)
            nc.sync.dma_start(table_words[:, cols].bitcast(I32), words_in_hbm[:, cols])
        load_scale_rows(table_planes, tab_scales)
        x_first = [load_rows("x_first%d" % n, x, n * PIECE, PIECE) for n in range(HALF // PIECE)]
        wz_raw = [load_rows("wz_raw0", wz, 0, PIECE)]
        uz_codes = load_words("uz_codes", uz_words)
        load_scale_rows(uz_planes, uz_scales)
        nc.sync.dma_start(bias_rows[0:CHUNKS, :], bz.rearrange("(c p) -> c p", p=P))
        nc.sync.dma_start(bias_rows[CHUNKS : 2 * CHUNKS, :], bn.rearrange("(c p) -> c p", p=P))
        x_second = load_rows("x_second", x, HALF, HALF)
        un_codes = load_words("un_codes", un_words)
        load_scale_rows(un_planes, un_scales)
        wn_raw = [load_rows("wn_raw0", wn, 0, PIECE)]
        weight = keep.tile([P, J], F32, name="weight")
        states = []
        for c in range(CHUNKS):
            state = keep.tile([P, T], F32, name="state%d" % c)
            nc.sync.dma_start(state[:], hT[c * P : (c + 1) * P, :])
            states.append(state)
            i = c // 2 + 1
            if c % 2 == 0 and i < N // PIECE:
                wz_raw.append(load_rows("wz_raw%d" % i, wz, i * PIECE, PIECE))
                wn_raw.append(load_rows("wn_raw%d" % i, wn, i * PIECE, PIECE))
            if c == 0:
                nc.sync.dma_start(weight[:], wgo)

        bias_bank = psum.tile([P, P], F32, name="bias_bank", tag="xn", bufs=3)
        nc.tensor.transpose(bias_bank[:], bias_rows[:], identity[:])
        bias_cols = keep.tile([P, 2 * CHUNKS], F32, name="bias_cols")
        nc.scalar.copy(bias_cols[:], bias_bank[:, : 2 * CHUNKS])

        halves = [slice(0, HALF), slice(HALF, J)]

        def look_up_table(h, plane_tags):
            part = offsets[:, h * HALF // LIST_ROWS : (h + 1) * HALF // LIST_ROWS]
            picked = keep.tile([P, HALF], U32, name="picked%d" % h)
            nc.vector.tensor_copy(picked[:], table_words[:].indirect(part))
            planes = []
            for a in range(STATE_PASSES):
                plane = keep.tile([P, HALF], U8, name="v_plane%d_%d" % (h, a), tag=plane_tags[a], align_bytes=64)
                nc.vector.tensor_copy(plane[:], table_planes[:, a, :].indirect(part))
                planes.append(plane)
            codes = keep.tile([P, STATE_PASSES, 2 * HALF], U8, name="v_codes%d" % h, align_bytes=64)
            nc.vector.tensor_copy(
                codes[:].bitcast(U16), picked[:].bitcast(U16).rearrange("p (j a) -> p a j", a=STATE_PASSES)
            )
            return codes, planes

        def quantise(name, raws, pool, tag):
            width = raws[0].shape[2]
            grouped = pool.tile(
                [P, len(raws), width, PACK], BF16, name="grouped_" + name, tag=tag, align_bytes=64, bufs=1
            )
            for n, raw in enumerate(raws):
                nc.scalar.copy(
                    grouped[:, n].rearrange("p (c s) i -> p c i s", s=4), raw[:].rearrange("p i (c s) -> p c i s", s=4)
                )
            codes = keep.tile([P, len(raws) * width], U32, name=name + "_codes", align_bytes=64)
            plane = keep.tile([P, len(raws) * width], U8, name=name + "_plane", align_bytes=64)
            nc.vector.quantize_mx(codes[:].bitcast(FP8X4), plane[:], grouped[:].rearrange("p n c i -> p (n c i)"))
            return codes, plane

        v_q = [look_up_table(0, ["v_plane0", "v_plane1"])]
        x_q = [quantise("x0", x_first, keep, "grouped_x0")]
        wz_q = [quantise("wz0", [wz_raw[0]], keep, "grouped_wz0") + (0,)]
        v_q.append(look_up_table(1, ["grouped_x0", "grouped_wz0"]))
        x_q.append(quantise("x1", [x_second], keep, "grouped_x1"))
        wn_q = [quantise("wn0", [wn_raw[0]], keep, "grouped_wn0") + (0,)]

        def quantise_weights(i, tag):
            both = quantise("w%d" % i, [wz_raw[i], wn_raw[i]], ring, tag)
            wz_q.append(both + (0,))
            wn_q.append(both + (PIECE,))

        def message_pass(bank, w_q, c, h, stop):
            codes, plane, first = w_q[c * P // PIECE]
            cols = slice(first + c * P % PIECE, first + c * P % PIECE + P)
            x_codes, x_plane = x_q[h]
            nc.tensor.matmul_mx(
                bank[:], codes[:, cols].bitcast(FP8X4), plane[:, cols], x_codes[:].bitcast(FP8X4), x_plane[:],
                start=True, stop=stop,
            )

        def state_passes(bank, u_codes, u_planes, c, h, start):
            v_codes, v_planes = v_q[h]
            for a in range(STATE_PASSES):
                nc.tensor.matmul_mx(
                    bank[:],
                    u_codes[:, a, 2 * c * P : 2 * (c + 1) * P].bitcast(FP4X4),
                    u_planes[:, a, c * P : (c + 1) * P],
                    v_codes[:, a, :].bitcast(FP4X4),
                    v_planes[a][:],
                    start=start and a == 0,
                    stop=a == STATE_PASSES - 1,
                )

        def products(c):
            if c == 0:
                gate = ring.tile([P, J], F32, name="gate0", tag="first", align_bytes=64, bufs=1)
            else:
                gate = ring.tile([P, J], F32, name="gate")
            gate_less_one = ring.tile([P, J], F32, name="gate_less_one")
            cand = ring.tile([P, J], F32, name="cand")
            hn_banks, xn_banks = [], []
            for h, cols in enumerate(halves):
                sz = psum.tile([P, HALF], F32, name="sz", bufs=2)
                message_pass(sz, wz_q, c, h, False)
                state_passes(sz, uz_codes, uz_planes, c, h, False)
                nc.scalar.activation(gate[:, cols], sz[:], ACT.Sigmoid, bias=bias_cols[:, c : c + 1])
                hn = psum.tile([P, HALF], F32, name="hn", bufs=3)
                state_passes(hn, un_codes, un_planes, c, h, True)
                xn = psum.tile([P, HALF], F32, name="xn", bufs=3)
                message_pass(xn, wn_q, c, h, True)
                hn_banks.append(hn)
                xn_banks.append(xn)
            return {"gate": gate, "gate_less_one": gate_less_one, "cand": cand, "hn": hn_banks, "xn": xn_banks}

        def lower_gate(chunk):
            nc.scalar.activation(chunk["gate_less_one"][:], chunk["gate"][:], ACT.Copy, bias=-1.0)

        def gate_hn(chunk, h):
            nc.vector.tensor_tensor(chunk["cand"][:, halves[h]], chunk["hn"][h][:], chunk["gate"][:, halves[h]], ALU.mult)

        def add_xn(chunk, h):
            nc.vector.tensor_tensor(chunk["cand"][:, halves[h]], chunk["xn"][h][:], chunk["cand"][:, halves[h]], ALU.add)

        def squash(chunk, c):
            bias = bias_cols[:, CHUNKS + c : CHUNKS + c + 1]
            nc.scalar.activation(chunk["cand"][:], chunk["cand"][:], ACT.Tanh, bias=bias)

        ahead = products(0)
        for h in range(2):
            gate_hn(ahead, h)
        for h in range(2):
            add_xn(ahead, h)
        lower_gate(ahead)
        squash(ahead, 0)

        for c in range(CHUNKS):
            gate_less_one, cand = ahead["gate_less_one"], ahead["cand"]
            more = c + 1 < CHUNKS
            next_piece = c // 2 + 1
            piece_due = c % 2 == 0 and next_piece < N // PIECE
            if piece_due and c > 0:
                quantise_weights(next_piece, "kept")
            if more:
                ahead = products(c + 1)
                lower_gate(ahead)
            if c == 0:
                quantise_weights(next_piece, "first")

            nc.vector.scalar_tensor_tensor(cand[:], gate_less_one[:], 1.0, cand[:], ALU.add, ALU.mult)
            kept = ring.tile([P, J], F32, name="kept", align_bytes=64, bufs=1)
            nc.vector.tensor_tensor(kept[:], states[c][:].indirect(offsets[:]), gate_less_one[:], ALU.mult)
            if more:
                gate_hn(ahead, 0)
                gate_hn(ahead, 1)
                add_xn(ahead, 0)
            if c == 0:
                blend = ring.tile([P, J], F32, name="blend0", tag="first", align_bytes=64, bufs=1)
            else:
                blend = ahead["gate"]
            nc.vector.tensor_tensor(blend[:], cand[:], kept[:], ALU.subtract)
            if more:
                add_xn(ahead, 1)
                squash(ahead, c + 1)

            page = pages[c % 2]
            nc.vector.tensor_tensor(page[:].indirect(offsets[:]), blend[:], weight[:], ALU.mult)
            nc.scalar.dma_start(out[c * P : (c + 1) * P, :], page[:])
